import numpy as np
import ml_dtypes


def mxq(x, axis, fmt="e4m3"):
    dtype, down = {"e4m3": (ml_dtypes.float8_e4m3fn, 7), "e5m2": (ml_dtypes.float8_e5m2, 14)}[fmt]
    v = np.moveaxis(np.asarray(x, np.float32).astype(ml_dtypes.bfloat16).astype(np.float64), axis, -1)
    blocks = v.reshape(v.shape[:-1] + (-1, 32))
    amax = np.abs(blocks).max(-1, keepdims=True)
    byte = np.maximum(np.where(amax > 0, np.frexp(amax)[1] - 1 + 127, 0) - down, 1)
    scale = np.exp2(byte - 127.0)
    codes = (blocks / scale).astype(np.float32).astype(dtype).astype(np.float64)
    return np.moveaxis((codes * scale).reshape(v.shape), -1, axis)


WIDE = False


def mx_kscale(k):
    if not WIDE:
        return np.ones(k)
    levels = np.array([10, -10, 5, -5, 0])
    if k % 512:
        return np.exp2(np.random.permutation(np.resize(levels, k // 32))).repeat(32)
    a = np.empty((k // 512, 16))
    for p in range(k // 512):
        a[p, :8] = np.random.permutation(np.resize(levels, 8))
        for g in range(8):
            far = levels[np.abs(levels - a[p, g]) >= 10]
            a[p, g + 8] = far[np.random.randint(len(far))]
    return np.exp2(a.ravel()).repeat(32)


def f64(x):
    return np.asarray(x).astype(np.float64)


def striped(idx):
    return np.tile(idx.reshape(-1, 16).T, (8, 1)).astype(np.uint16)


def unstriped(offs):
    return offs[:16].T.reshape(-1).astype(np.int64)


E2M1 = np.array([0.0, 0.5, 1.0, 1.5, 2.0, 3.0, 4.0, 6.0, -0.0, -0.5, -1.0, -1.5, -2.0, -3.0, -4.0, -6.0])


def pack_weight(w, fmt):
    k, n = w.shape
    w = f64(np.asarray(w, np.float32).astype(ml_dtypes.bfloat16)).reshape(k // 32, 32, n)
    amax = np.abs(w).max(1)
    if fmt == "e4m3":
        byte = np.frexp(amax)[1] - 1 + 127 - 7
    else:
        mant, ex = np.frexp(amax / 6.0)
        byte = np.where(mant > 0.5, ex, ex - 1) + 127
    byte = np.clip(np.where(amax > 0, byte, 1), 1, 254)
    scaled = (w * np.exp2(127.0 - byte)[:, None, :]).reshape(k, n).astype(np.float32)
    by_word = np.ascontiguousarray(scaled.reshape(k // 512, 128, 4, n).transpose(0, 1, 3, 2))
    if fmt == "e4m3":
        words = by_word.astype(ml_dtypes.float8_e4m3fn).view(np.uint8)
    else:
        c = by_word.astype(ml_dtypes.float4_e2m1fn).view(np.uint8) & 0xF
        words = (c[..., 0::2] | (c[..., 1::2] << 4)).reshape(k // 512, 128, 2 * n)
    return np.ascontiguousarray(words), np.ascontiguousarray(byte.astype(np.uint8).reshape(k // 512, 16, n))


def unpack_weight(words, scales, fmt):
    g, _, n = scales.shape
    words = np.ascontiguousarray(words).reshape(g, 128, n, -1)
    if fmt == "e4m3":
        vals = words.view(ml_dtypes.float8_e4m3fn).astype(np.float64)
    else:
        nib = np.empty((g, 128, n, 4), np.uint8)
        nib[..., 0::2] = words & 0xF
        nib[..., 1::2] = words >> 4
        vals = E2M1[nib]
    vals = vals * np.repeat(np.exp2(scales.astype(np.float64) - 127.0), 8, axis=1)[..., None]
    return vals.transpose(0, 1, 3, 2).reshape(g * 512, n)


def gelu(v):
    return 0.5 * v * (1.0 + np.tanh(np.sqrt(2.0 / np.pi) * (v + 0.044715 * v**3)))


K, H, T, S, T2, P = 1024, 512, 4096, 1024, 2048, 1024

def setup_inputs():
    n = np.random.standard_normal
    s, u = mx_kscale(K)[:, None], mx_kscale(H)[:, None]
    d = {}
    d["tab_words"], d["tab_scales"] = pack_weight(n((K, T)) * s, "e4m3")
    d["offs"] = striped(np.random.permutation(T)[:S])
    d["offs2"] = striped(np.random.permutation(T2)[:S])
    d["offs3"] = striped(np.random.permutation(T2)[:P])
    d["offs4"] = striped(np.random.permutation(T2)[:P])
    d["w1"] = (n((K, H)) / K ** 0.5 / s * u.T).astype(np.float32)
    d["w2_words"], d["w2_scales"] = pack_weight(n((K, H)) / K ** 0.5 / s * u.T, "e2m1")
    d["w3"] = (n((K, H)) / K ** 0.5 / s * u.T).astype(np.float32)
    d["wgs"] = np.exp(0.3 * n((128, S))).astype(np.float32)
    d["page0"] = (1.2 * n((H, T2)) * u).astype(np.float32)
    d["sc"] = (np.exp(0.3 * n(H)) / u[:, 0]).astype(np.float32)
    d["gain"] = (1.4 * np.exp(0.3 * n(H)) * u[:, 0]).astype(np.float32)
    d["w4_words"], d["w4_scales"] = pack_weight(n((H, H)) / H ** 0.5 / u, "e2m1")
    return d

def reference(tab_words, tab_scales, offs, offs2, offs3, offs4, w1, w2_words, w2_scales, w3, wgs, page0, sc, gain, w4_words, w4_scales):
    v = unpack_weight(tab_words, tab_scales, "e4m3")[:, unstriped(offs)]
    a1 = mxq(f64(w1), 0, "e4m3").T @ v
    a2 = unpack_weight(w2_words, w2_scales, "e2m1").T @ v
    a3 = mxq(f64(w3), 0, "e4m3").T @ v
    h = np.maximum(a1, a2) - a3
    page = f64(page0).copy()
    page[:, unstriped(offs2)] = np.tile(f64(wgs), (H // 128, 1)) * h
    page = page * f64(sc)[:, None]
    x = np.tanh(page[:, unstriped(offs3)]) * f64(gain)[:, None]
    y = unpack_weight(w4_words, w4_scales, "e2m1").T @ mxq(x, 0, "e4m3")
    out = y - np.abs(page[:, unstriped(offs4)])
    return out

@@ -1,0 +1,272 @@
+from contextlib import ExitStack
+
+import concourse.mybir as mybir
+from concourse.masks import make_identity
+
+K, H, T, S, T2, M = 1024, 512, 4096, 1024, 2048, 1024
+FLOPS = 3 * 2 * K * H * S + 2 * H * H * M
+
+F32 = mybir.dt.float32
+BF16 = mybir.dt.bfloat16
+I32 = mybir.dt.int32
+U32 = mybir.dt.uint32
+U16 = mybir.dt.uint16
+U8 = mybir.dt.uint8
+FP8X4 = mybir.dt.float8_e4m3fn_x4
+FP4X4 = mybir.dt.float4_e2m1fn_x4
+ALU = mybir.AluOpType
+ACT = mybir.ActivationFunctionType
+
+P = 128
+PACK = 4
+PASSES = K // (P * PACK)
+QUADS = 4
+ROW_TILES = H // P
+HALF = 512
+LIST_COLS = HALF // 16
+UNITS = 2 * ROW_TILES
+
+
+def tile_list_trap_catch_board_kernel(
+    tc, tab_words, tab_scales, offs, offs2, offs3, offs4, w1, w2_words, w2_scales, w3, wgs, page0, sc, gain,
+    w4_words, w4_scales, out,
+):
+    nc = tc.nc
+    with ExitStack() as ctx:
+        keep = ctx.enter_context(tc.tile_pool(name="keep", bufs=1))
+        ring = ctx.enter_context(tc.tile_pool(name="ring", bufs=2))
+        psum = ctx.enter_context(tc.psum_pool(name="psum", bufs=2))
+
+        idx_tab = keep.tile([P, S // 16], U16, name="idx_tab")
+        idx_put = keep.tile([P, S // 16], U16, name="idx_put")
+        idx_due = keep.tile([P, M // 16], U16, name="idx_due")
+        idx_ctl = keep.tile([P, M // 16], U16, name="idx_ctl")
+
+        tab_w = [keep.tile([P, T], I32, name=f"tab_w{a}") for a in range(PASSES)]
+        tab_s = keep.tile([P, PASSES * T], U8, name="tab_s")
+        v_w = [keep.tile([P, S], U32, name=f"v_w{a}", align_bytes=64) for a in range(PASSES)]
+        v_s = [keep.tile([P, S], U8, name=f"v_s{a}", align_bytes=64) for a in range(PASSES)]
+        w2_w = keep.tile([P, PASSES * 2 * H], U8, name="w2_w", align_bytes=64)
+        w2_s = keep.tile([P, PASSES * H], U8, name="w2_s", align_bytes=64)
+        w4_w = keep.tile([P, 2 * H], U8, name="w4_w", align_bytes=64)
+        w4_s = keep.tile([P, H], U8, name="w4_s", align_bytes=64)
+        raw = [keep.tile([P, 2 * PASSES * PACK * P], F32, name=f"raw{q}") for q in range(ROW_TILES)]
+        w_c = [keep.tile([P, 2 * PASSES * P], U32, name=f"w_c{q}", align_bytes=64) for q in range(ROW_TILES)]
+        w_s = [keep.tile([P, 2 * PASSES * P], U8, name=f"w_s{q}", align_bytes=64) for q in range(ROW_TILES)]
+        page = [keep.tile([P, T2], F32, name=f"page{q}") for q in range(ROW_TILES)]
+        wgs_t = keep.tile([P, S], F32, name="wgs_t", tag="wide")
+        sc_t = keep.tile([P, ROW_TILES], F32, name="sc_t")
+        gain_t = keep.tile([P, ROW_TILES], F32, name="gain_t")
+        ident = keep.tile([P, P], F32, name="ident")
+        due = [keep.tile([P, M], F32, name=f"due{q}") for q in range(ROW_TILES)]
+        bounded = [keep.tile([P, M], F32, name=f"bounded{q}") for q in range(ROW_TILES)]
+        x_rows = [keep.tile([P, PACK, HALF], BF16, name=f"x_rows{hf}", tag=f"x_rows{hf}") for hf in range(2)]
+
+        def half(hf):
+            return slice(hf * HALF, (hf + 1) * HALF)
+
+        def list_half(idx, hf):
+            return idx[:, hf * LIST_COLS : (hf + 1) * LIST_COLS]
+
+        def load_scale_rows(queue, plane, scales):
+            rows = plane[:].bitcast(I32).rearrange("p (a c) -> p a c", a=scales.shape[0])
+            for quad in range(QUADS):
+                src = scales[:, 4 * quad : 4 * quad + 4, :].bitcast(I32).rearrange("a r c -> r a c")
+                queue.dma_start(out=rows[32 * quad : 32 * quad + 4], in_=src)
+
+        def load_weights(q):
+            for n, w in enumerate((w1, w3)):
+                for a in range(PASSES):
+                    src = w[a * P * PACK : (a + 1) * P * PACK, q * P : (q + 1) * P]
+                    c0 = (n * PASSES + a) * PACK * P
+                    dst = raw[q][:, c0 : c0 + PACK * P].rearrange("p (i r) -> p i r", i=PACK)
+                    nc.sync.dma_start(out=dst, in_=src.rearrange("(p i) r -> p i r", i=PACK))
+
+        def load_table(a):
+            nc.sync.dma_start(out=tab_w[a][:], in_=tab_words[a].rearrange("p t i -> p (t i)").bitcast(I32))
+
+        def load_page(q):
+            nc.sync.dma_start(out=page[q][:], in_=page0[q * P : (q + 1) * P, :])
+
+        nc.vector.memset(tab_s[:].bitcast(I32), 0)
+        nc.gpsimd.memset(w2_s[:].bitcast(I32), 0)
+        nc.gpsimd.memset(w4_s[:].bitcast(I32), 0)
+        load_scale_rows(nc.gpsimd, w2_s, w2_scales)
+        nc.sync.dma_start(idx_tab[:], offs)
+        load_table(0)
+        load_scale_rows(nc.sync, tab_s, tab_scales)
+        load_table(1)
+        nc.sync.dma_start(
+            out=w2_w[:].bitcast(I32).rearrange("p (a c) -> p a c", a=PASSES),
+            in_=w2_words.bitcast(I32).rearrange("a p c -> p a c"),
+        )
+        load_weights(0)
+        nc.sync.dma_start(out=wgs_t[:, half(0)], in_=wgs[:, half(0)])
+        nc.sync.dma_start(idx_put[:], offs2)
+        load_page(0)
+        load_weights(1)
+        with nc.allow_non_contiguous_dma(reason="one value of sc and of gain for each partition"):
+            nc.sync.dma_start(out=sc_t[:], in_=sc.rearrange("(q p) -> p q", p=P))
+            nc.sync.dma_start(out=gain_t[:], in_=gain.rearrange("(q p) -> p q", p=P))
+        nc.sync.dma_start(out=wgs_t[:, half(1)], in_=wgs[:, half(1)])
+        nc.sync.dma_start(idx_due[:], offs3)
+        for q in range(1, ROW_TILES):
+            load_page(q)
+            if q + 1 < ROW_TILES:
+                load_weights(q + 1)
+        nc.sync.dma_start(idx_ctl[:], offs4)
+        nc.sync.dma_start(out=w4_w[:].bitcast(I32), in_=w4_words[0].bitcast(I32))
+        make_identity(nc, ident[:])
+        load_scale_rows(nc.gpsimd, w4_s, w4_scales)
+
+        def quantize_weights(q, pieces):
+            grouped = ring.tile([P, 2 * PASSES * P * PACK], BF16, name="grouped", align_bytes=64)
+            count = 2 * PASSES // pieces
+            for first in range(0, 2 * PASSES, count):
+                values = slice(first * PACK * P, (first + count) * PACK * P)
+                words = slice(first * P, (first + count) * P)
+                nc.scalar.copy(
+                    out=grouped[:, values].rearrange("p (n c k i) -> p n c i k", n=count, k=4, i=PACK),
+                    in_=raw[q][:, values].rearrange("p (n i c k) -> p n c i k", n=count, k=4, i=PACK),
+                )
+                nc.vector.quantize_mx(
+                    out=w_c[q][:, words].bitcast(FP8X4), scales=w_s[q][:, words], in_=grouped[:, values]
+                )
+
+        def gather_words(a, hf):
+            nc.vector.tensor_copy(v_w[a][:, half(hf)], tab_w[a][:].bitcast(U32).indirect(list_half(idx_tab, hf)))
+
+        def gather_scales(a, hf):
+            nc.vector.tensor_copy(v_s[a][:, half(hf)], tab_s[:, a * T : (a + 1) * T].indirect(list_half(idx_tab, hf)))
+
+        for hf in range(2):
+            for a in range(PASSES):
+                gather_words(a, hf)
+                gather_scales(a, hf)
+            if hf == 0:
+                quantize_weights(0, 2 * PASSES)
+
+        def product(u, tag, moving):
+            hf = u % 2
+            bank = psum.tile([P, HALF], F32, name=tag, tag=tag)
+            for a in range(PASSES):
+                codes, scales = moving(a)
+                for jt in range(HALF // P):
+                    cols = slice(hf * HALF + jt * P, hf * HALF + (jt + 1) * P)
+                    nc.tensor.matmul_mx(
+                        out=bank[:, jt * P : (jt + 1) * P],
+                        lhsT=v_w[a][:, cols].bitcast(FP8X4),
+                        lhsT_scale=v_s[a][:, cols],
+                        rhs=codes,
+                        rhs_scale=scales,
+                        start=(a == 0 and jt == 0),
+                        stop=(a == PASSES - 1 and jt == HALF // P - 1),
+                    )
+            return bank
+
+        def first_stage(u):
+            q = u // 2
+
+            def quantised(n):
+                def moving(a):
+                    cols = slice((n * PASSES + a) * P, (n * PASSES + a + 1) * P)
+                    return w_c[q][:, cols].bitcast(FP8X4), w_s[q][:, cols]
+
+                return moving
+
+            def packed(a):
+                c0 = a * H + q * P
+                return w2_w[:, 2 * c0 : 2 * (c0 + P)].bitcast(FP4X4), w2_s[:, c0 : c0 + P]
+
+            if u % 2 == 0 and q > 0:
+                a2_sb = due[q - 1][:, half(0)]
+                a3_sb = bounded[q - 1][:, half(0)]
+            else:
+                a2_sb = ring.tile([P, HALF], F32, name="a2_sb")[:]
+                a3_sb = ring.tile([P, HALF], F32, name="a3_sb")[:]
+            a2 = product(u, "a2", packed)
+            a1 = product(u, "a1", quantised(0))
+            a3 = product(u, "a3", quantised(1))
+            larger = ring.tile([P, HALF], F32, name="larger")
+            nc.scalar.copy(out=a2_sb, in_=a2[:])
+            nc.vector.tensor_tensor(larger[:], a1[:], a2_sb, ALU.max)
+            nc.scalar.activation(a3_sb, a3[:], ACT.Copy, scale=-1.0)
+            return larger[:], a3_sb
+
+        def put(u, terms):
+            q, hf = divmod(u, 2)
+            bank = psum.tile([P, HALF], F32, name="h", tag="h")
+            for n, term in enumerate(terms if u == 0 else reversed(terms)):
+                for jt in range(HALF // P):
+                    cols = slice(jt * P, (jt + 1) * P)
+                    nc.tensor.matmul(
+                        bank[:, cols], term[:, cols], ident[:], is_transpose=True,
+                        start=(n == 0 and jt == 0), stop=(n == 1 and jt == HALF // P - 1),
+                    )
+            if hf == 1 and q + 1 < ROW_TILES:
+                h = raw[q + 1][:, 0:HALF]
+            else:
+                h = ring.tile([P, HALF], F32, name="h_sb")[:]
+            nc.scalar.copy(out=h, in_=bank[:])
+            nc.vector.tensor_tensor(page[q][:].indirect(list_half(idx_put, hf)), h, wgs_t[:, half(hf)], ALU.mult)
+
+        def fetch_due(q, cols, idx):
+            nc.vector.tensor_copy(due[q][:, cols], page[q][:].indirect(idx))
+
+        def bound(q, cols):
+            x_nat = ring.tile([P, M], BF16, name="x_nat")
+            nc.scalar.activation(bounded[q][:, cols], due[q][:, cols], ACT.Tanh, scale=sc_t[:, q : q + 1])
+            nc.scalar.activation(x_nat[:, cols], bounded[q][:, cols], ACT.Copy, scale=gain_t[:, q : q + 1])
+            for hf in range(cols.start // HALF, cols.stop // HALF):
+                for i in range(PACK):
+                    nc.sync.dma_start(out=x_rows[hf][32 * q : 32 * (q + 1), i, :], in_=x_nat[i:P:PACK, half(hf)])
+
+        terms = first_stage(0)
+        for u in range(UNITS):
+            q, hf = divmod(u, 2)
+            if hf == (1 if q == 0 else 0) and q + 1 < ROW_TILES:
+                quantize_weights(q + 1, 1)
+            ahead = first_stage(u + 1) if u + 1 < UNITS else None
+            put(u, terms)
+            terms = ahead
+            if hf == 1 and q + 1 < ROW_TILES:
+                fetch_due(q, slice(0, M), idx_due[:])
+            if hf == 0 and q > 0:
+                bound(q - 1, slice(0, M))
+        for hf in range(2):
+            fetch_due(ROW_TILES - 1, half(hf), list_half(idx_due, hf))
+            bound(ROW_TILES - 1, half(hf))
+
+        control = keep.tile([P, 2 * ROW_TILES, HALF], F32, name="control", tag="wide")
+        x_c, x_s = [], []
+        for hf in range(2):
+            x_grouped = ring.tile([P, HALF, PACK], BF16, name="grouped", align_bytes=64)
+            nc.scalar.copy(
+                out=x_grouped[:].rearrange("p (c k) i -> p c i k", k=4),
+                in_=x_rows[hf][:].rearrange("p i (c k) -> p c i k", k=4),
+            )
+            x_c.append(ring.tile([P, HALF], U32, name="x_c", align_bytes=64))
+            x_s.append(ring.tile([P, HALF], U8, name="x_s", align_bytes=64))
+            nc.vector.quantize_mx(
+                out=x_c[hf][:].bitcast(FP8X4), scales=x_s[hf][:], in_=x_grouped[:].rearrange("p c i -> p (c i)")
+            )
+        sizes = keep.tile([P, 2 * ROW_TILES, HALF], F32, name="sizes", tag="x_rows0")
+        for hf in range(2):
+            for q in range(ROW_TILES):
+                picked = control[:, hf * ROW_TILES + q, :]
+                nc.vector.tensor_copy(picked, page[q][:].indirect(list_half(idx_ctl, hf)))
+                size = sizes[:, hf * ROW_TILES + q, :]
+                nc.scalar.activation(size, picked, ACT.Abs, scale=sc_t[:, q : q + 1])
+                tag = ("a2", "a1", "a3", "h")[q]
+                y = psum.tile([P, HALF], F32, name=tag, tag=tag)
+                nc.tensor.matmul_mx(
+                    out=y[:],
+                    lhsT=w4_w[:, 2 * q * P : 2 * (q + 1) * P].bitcast(FP4X4),
+                    lhsT_scale=w4_s[:, q * P : (q + 1) * P],
+                    rhs=x_c[hf][:].bitcast(FP8X4),
+                    rhs_scale=x_s[hf][:],
+                    start=True,
+                    stop=True,
+                )
+                nc.vector.tensor_tensor(picked, y[:], size, ALU.subtract)
+                nc.sync.dma_start(out=out[q * P : (q + 1) * P, half(hf)], in_=picked)

@@ -55,8 +55,10 @@ def tile_list_trap_catch_board_kernel(
         w_s = [keep.tile([P, 2 * PASSES * P], U8, name=f"w_s{q}", align_bytes=64) for q in range(ROW_TILES)]
         page = [keep.tile([P, T2], F32, name=f"page{q}") for q in range(ROW_TILES)]
         wgs_t = keep.tile([P, S], F32, name="wgs_t", tag="wide")
-        sc_t = keep.tile([P, ROW_TILES], F32, name="sc_t")
-        gain_t = keep.tile([P, ROW_TILES], F32, name="gain_t")
+        factor_rows = keep.tile([P, P], F32, name="factor_rows")
+        factors = keep.tile([P, 2 * ROW_TILES], F32, name="factors")
+        sc_t = factors[:, 0:ROW_TILES]
+        gain_t = factors[:, ROW_TILES : 2 * ROW_TILES]
         ident = keep.tile([P, P], F32, name="ident")
         due = [keep.tile([P, M], F32, name=f"due{q}") for q in range(ROW_TILES)]
         bounded = [keep.tile([P, M], F32, name=f"bounded{q}") for q in range(ROW_TILES)]
@@ -91,6 +93,8 @@ def tile_list_trap_catch_board_kernel(
         nc.vector.memset(tab_s[:].bitcast(I32), 0)
         nc.gpsimd.memset(w2_s[:].bitcast(I32), 0)
         nc.gpsimd.memset(w4_s[:].bitcast(I32), 0)
+        nc.gpsimd.memset(factor_rows[:], 0.0)
+        make_identity(nc, ident[:])
         load_scale_rows(nc.gpsimd, w2_s, w2_scales)
         nc.sync.dma_start(idx_tab[:], offs)
         load_table(0)
@@ -105,19 +109,17 @@ def tile_list_trap_catch_board_kernel(
         nc.sync.dma_start(idx_put[:], offs2)
         load_page(0)
         load_weights(1)
-        with nc.allow_non_contiguous_dma(reason="one value of sc and of gain for each partition"):
-            nc.sync.dma_start(out=sc_t[:], in_=sc.rearrange("(q p) -> p q", p=P))
-            nc.sync.dma_start(out=gain_t[:], in_=gain.rearrange("(q p) -> p q", p=P))
         nc.sync.dma_start(out=wgs_t[:, half(1)], in_=wgs[:, half(1)])
         nc.sync.dma_start(idx_due[:], offs3)
+        nc.sync.dma_start(out=factor_rows[0:ROW_TILES, :], in_=sc.rearrange("(q p) -> q p", p=P))
+        nc.sync.dma_start(out=factor_rows[ROW_TILES : 2 * ROW_TILES, :], in_=gain.rearrange("(q p) -> q p", p=P))
         for q in range(1, ROW_TILES):
-            load_page(q)
             if q + 1 < ROW_TILES:
                 load_weights(q + 1)
+            load_page(q)
         nc.sync.dma_start(idx_ctl[:], offs4)
         nc.sync.dma_start(out=w4_w[:].bitcast(I32), in_=w4_words[0].bitcast(I32))
-        make_identity(nc, ident[:])
-        load_scale_rows(nc.gpsimd, w4_s, w4_scales)
+        load_scale_rows(nc.sync, w4_s, w4_scales)
 
         def quantize_weights(q, pieces):
             grouped = ring.tile([P, 2 * PASSES * P * PACK], BF16, name="grouped", align_bytes=64)
@@ -151,6 +153,17 @@ def tile_list_trap_catch_board_kernel(
             bank = psum.tile([P, HALF], F32, name=tag, tag=tag)
             for a in range(PASSES):
                 codes, scales = moving(a)
+                if u == 0:
+                    nc.tensor.matmul_mx(
+                        out=bank[:],
+                        lhsT=codes,
+                        lhsT_scale=scales,
+                        rhs=v_w[a][:, half(hf)].bitcast(FP8X4),
+                        rhs_scale=v_s[a][:, half(hf)],
+                        start=(a == 0),
+                        stop=(a == PASSES - 1),
+                    )
+                    continue
                 for jt in range(HALF // P):
                     cols = slice(hf * HALF + jt * P, hf * HALF + (jt + 1) * P)
                     nc.tensor.matmul_mx(
@@ -190,13 +203,16 @@ def tile_list_trap_catch_board_kernel(
             larger = ring.tile([P, HALF], F32, name="larger")
             nc.scalar.copy(out=a2_sb, in_=a2[:])
             nc.vector.tensor_tensor(larger[:], a1[:], a2_sb, ALU.max)
+            if u == 0:
+                nc.vector.tensor_tensor(a3_sb, larger[:], a3[:], ALU.subtract)
+                return a3_sb
             nc.scalar.activation(a3_sb, a3[:], ACT.Copy, scale=-1.0)
-            return larger[:], a3_sb
+            return a3_sb, larger[:]
 
-        def put(u, terms):
+        def turn(u, terms):
             q, hf = divmod(u, 2)
             bank = psum.tile([P, HALF], F32, name="h", tag="h")
-            for n, term in enumerate(terms if u == 0 else reversed(terms)):
+            for n, term in enumerate(terms):
                 for jt in range(HALF // P):
                     cols = slice(jt * P, (jt + 1) * P)
                     nc.tensor.matmul(
@@ -208,6 +224,10 @@ def tile_list_trap_catch_board_kernel(
             else:
                 h = ring.tile([P, HALF], F32, name="h_sb")[:]
             nc.scalar.copy(out=h, in_=bank[:])
+            return h
+
+        def put(u, h):
+            q, hf = divmod(u, 2)
             nc.vector.tensor_tensor(page[q][:].indirect(list_half(idx_put, hf)), h, wgs_t[:, half(hf)], ALU.mult)
 
         def fetch_due(q, cols, idx):
@@ -227,7 +247,11 @@ def tile_list_trap_catch_board_kernel(
             if hf == (1 if q == 0 else 0) and q + 1 < ROW_TILES:
                 quantize_weights(q + 1, 1)
             ahead = first_stage(u + 1) if u + 1 < UNITS else None
-            put(u, terms)
+            put(u, terms if u == 0 else turn(u, terms))
+            if u == 1:
+                turned = psum.tile([P, HALF], F32, name="h", tag="h")
+                nc.tensor.transpose(turned[:, 0:P], factor_rows[:], ident[:])
+                nc.scalar.copy(out=factors[:], in_=turned[:, 0 : 2 * ROW_TILES])
             terms = ahead
             if hf == 1 and q + 1 < ROW_TILES:
                 fetch_due(q, slice(0, M), idx_due[:])

@@ -50,7 +50,7 @@ def tile_list_trap_catch_board_kernel(
         w2_s = keep.tile([P, PASSES * H], U8, name="w2_s", align_bytes=64)
         w4_w = keep.tile([P, 2 * H], U8, name="w4_w", align_bytes=64)
         w4_s = keep.tile([P, H], U8, name="w4_s", align_bytes=64)
-        raw = [keep.tile([P, 2 * PASSES * PACK * P], F32, name=f"raw{q}") for q in range(ROW_TILES)]
+        raw = {}
         w_c = [keep.tile([P, 2 * PASSES * P], U32, name=f"w_c{q}", align_bytes=64) for q in range(ROW_TILES)]
         w_s = [keep.tile([P, 2 * PASSES * P], U8, name=f"w_s{q}", align_bytes=64) for q in range(ROW_TILES)]
         page = [keep.tile([P, T2], F32, name=f"page{q}") for q in range(ROW_TILES)]
@@ -76,13 +76,13 @@ def tile_list_trap_catch_board_kernel(
                 src = scales[:, 4 * quad : 4 * quad + 4, :].bitcast(I32).rearrange("a r c -> r a c")
                 queue.dma_start(out=rows[32 * quad : 32 * quad + 4], in_=src)
 
-        def load_weights(q):
-            for n, w in enumerate((w1, w3)):
-                for a in range(PASSES):
-                    src = w[a * P * PACK : (a + 1) * P * PACK, q * P : (q + 1) * P]
-                    c0 = (n * PASSES + a) * PACK * P
-                    dst = raw[q][:, c0 : c0 + PACK * P].rearrange("p (i r) -> p i r", i=PACK)
-                    nc.sync.dma_start(out=dst, in_=src.rearrange("(p i) r -> p i r", i=PACK))
+        def load_weight(n, first, count):
+            for a in range(PASSES):
+                staged = keep.tile([P, PACK, count * P], F32, name=f"raw{n}_{a}_{first}")
+                src = (w1, w3)[n][a * P * PACK : (a + 1) * P * PACK, first * P : (first + count) * P]
+                nc.sync.dma_start(out=staged[:], in_=src.rearrange("(p i) r -> p i r", i=PACK))
+                for q in range(count):
+                    raw[n, a, first + q] = staged[:, :, q * P : (q + 1) * P]
 
         def load_table(a):
             nc.sync.dma_start(out=tab_w[a][:], in_=tab_words[a].rearrange("p t i -> p (t i)").bitcast(I32))
@@ -95,7 +95,6 @@ def tile_list_trap_catch_board_kernel(
         nc.gpsimd.memset(w4_s[:].bitcast(I32), 0)
         nc.gpsimd.memset(factor_rows[:], 0.0)
         make_identity(nc, ident[:])
-        load_scale_rows(nc.gpsimd, w2_s, w2_scales)
         nc.sync.dma_start(idx_tab[:], offs)
         load_table(0)
         load_scale_rows(nc.sync, tab_s, tab_scales)
@@ -104,36 +103,37 @@ def tile_list_trap_catch_board_kernel(
             out=w2_w[:].bitcast(I32).rearrange("p (a c) -> p a c", a=PASSES),
             in_=w2_words.bitcast(I32).rearrange("a p c -> p a c"),
         )
-        load_weights(0)
+        load_scale_rows(nc.sync, w2_s, w2_scales)
+        load_weight(0, 0, 2)
+        load_weight(1, 0, 1)
         nc.sync.dma_start(out=wgs_t[:, half(0)], in_=wgs[:, half(0)])
         nc.sync.dma_start(idx_put[:], offs2)
         load_page(0)
-        load_weights(1)
+        load_weight(1, 1, 1)
         nc.sync.dma_start(out=wgs_t[:, half(1)], in_=wgs[:, half(1)])
         nc.sync.dma_start(idx_due[:], offs3)
         nc.sync.dma_start(out=factor_rows[0:ROW_TILES, :], in_=sc.rearrange("(q p) -> q p", p=P))
         nc.sync.dma_start(out=factor_rows[ROW_TILES : 2 * ROW_TILES, :], in_=gain.rearrange("(q p) -> q p", p=P))
         for q in range(1, ROW_TILES):
             if q + 1 < ROW_TILES:
-                load_weights(q + 1)
+                load_weight(0, q + 1, 1)
+                load_weight(1, q + 1, 1)
             load_page(q)
         nc.sync.dma_start(idx_ctl[:], offs4)
         nc.sync.dma_start(out=w4_w[:].bitcast(I32), in_=w4_words[0].bitcast(I32))
         load_scale_rows(nc.sync, w4_s, w4_scales)
 
-        def quantize_weights(q, pieces):
-            grouped = ring.tile([P, 2 * PASSES * P * PACK], BF16, name="grouped", align_bytes=64)
-            count = 2 * PASSES // pieces
-            for first in range(0, 2 * PASSES, count):
-                values = slice(first * PACK * P, (first + count) * PACK * P)
-                words = slice(first * P, (first + count) * P)
+        def quantize_weights(q, first, count):
+            grouped = ring.tile([P, count * P * PACK], BF16, name="grouped", align_bytes=64, bufs=3)
+            for piece in range(count):
+                n, a = divmod(first + piece, PASSES)
+                values = grouped[:, piece * PACK * P : (piece + 1) * PACK * P]
                 nc.scalar.copy(
-                    out=grouped[:, values].rearrange("p (n c k i) -> p n c i k", n=count, k=4, i=PACK),
-                    in_=raw[q][:, values].rearrange("p (n i c k) -> p n c i k", n=count, k=4, i=PACK),
+                    out=values.rearrange("p (c k i) -> p c i k", k=4, i=PACK),
+                    in_=raw[n, a, q].rearrange("p i (c k) -> p c i k", k=4),
                 )
-                nc.vector.quantize_mx(
-                    out=w_c[q][:, words].bitcast(FP8X4), scales=w_s[q][:, words], in_=grouped[:, values]
-                )
+            words = slice(first * P, (first + count) * P)
+            nc.vector.quantize_mx(out=w_c[q][:, words].bitcast(FP8X4), scales=w_s[q][:, words], in_=grouped[:])
 
         def gather_words(a, hf):
             nc.vector.tensor_copy(v_w[a][:, half(hf)], tab_w[a][:].bitcast(U32).indirect(list_half(idx_tab, hf)))
@@ -146,7 +146,8 @@ def tile_list_trap_catch_board_kernel(
                 gather_words(a, hf)
                 gather_scales(a, hf)
             if hf == 0:
-                quantize_weights(0, 2 * PASSES)
+                for piece in range(2 * PASSES):
+                    quantize_weights(0, piece, 1)
 
         def product(u, tag, moving):
             hf = u % 2
@@ -194,6 +195,9 @@ def tile_list_trap_catch_board_kernel(
             if u % 2 == 0 and q > 0:
                 a2_sb = due[q - 1][:, half(0)]
                 a3_sb = bounded[q - 1][:, half(0)]
+            elif q == 0:
+                a2_sb = raw[1, u, 0].rearrange("p i r -> p (i r)")
+                a3_sb = ring.tile([P, HALF], F32, name="a3_sb")[:]
             else:
                 a2_sb = ring.tile([P, HALF], F32, name="a2_sb")[:]
                 a3_sb = ring.tile([P, HALF], F32, name="a3_sb")[:]
@@ -220,7 +224,7 @@ def tile_list_trap_catch_board_kernel(
                         start=(n == 0 and jt == 0), stop=(n == 1 and jt == HALF // P - 1),
                     )
             if hf == 1 and q + 1 < ROW_TILES:
-                h = raw[q + 1][:, 0:HALF]
+                h = raw[1, PASSES - 1, q + 1].rearrange("p i r -> p (i r)")
             else:
                 h = ring.tile([P, HALF], F32, name="h_sb")[:]
             nc.scalar.copy(out=h, in_=bank[:])
@@ -244,8 +248,10 @@ def tile_list_trap_catch_board_kernel(
         terms = first_stage(0)
         for u in range(UNITS):
             q, hf = divmod(u, 2)
-            if hf == (1 if q == 0 else 0) and q + 1 < ROW_TILES:
-                quantize_weights(q + 1, 1)
+            if q == 0:
+                quantize_weights(1, hf * PASSES, PASSES)
+            elif hf == 0 and q + 1 < ROW_TILES:
+                quantize_weights(q + 1, 0, 2 * PASSES)
             ahead = first_stage(u + 1) if u + 1 < UNITS else None
             put(u, terms if u == 0 else turn(u, terms))
             if u == 1:
@@ -264,7 +270,7 @@ def tile_list_trap_catch_board_kernel(
         control = keep.tile([P, 2 * ROW_TILES, HALF], F32, name="control", tag="wide")
         x_c, x_s = [], []
         for hf in range(2):
-            x_grouped = ring.tile([P, HALF, PACK], BF16, name="grouped", align_bytes=64)
+            x_grouped = ring.tile([P, HALF, PACK], BF16, name="grouped", align_bytes=64, bufs=3)
             nc.scalar.copy(
                 out=x_grouped[:].rearrange("p (c k) i -> p c i k", k=4),
                 in_=x_rows[hf][:].rearrange("p i (c k) -> p c i k", k=4),

@@ -20,11 +20,14 @@ ACT = mybir.ActivationFunctionType
 P = 128
 PACK = 4
 PASSES = K // (P * PACK)
-QUADS = 4
+QUADRANT = 32
+SCALE_ROWS = 4
 ROW_TILES = H // P
 HALF = 512
 LIST_COLS = HALF // 16
 UNITS = 2 * ROW_TILES
+PIECES = 2 * PASSES
+RUN = 4
 
 
 def tile_list_trap_catch_board_kernel(
@@ -50,11 +53,11 @@ def tile_list_trap_catch_board_kernel(
         w2_s = keep.tile([P, PASSES * H], U8, name="w2_s", align_bytes=64)
         w4_w = keep.tile([P, 2 * H], U8, name="w4_w", align_bytes=64)
         w4_s = keep.tile([P, H], U8, name="w4_s", align_bytes=64)
+        w_c = [keep.tile([P, PIECES * P], U32, name=f"w_c{q}", align_bytes=64) for q in range(ROW_TILES)]
+        w_s = [keep.tile([P, PIECES * P], U8, name=f"w_s{q}", align_bytes=64) for q in range(ROW_TILES)]
         raw = {}
-        w_c = [keep.tile([P, 2 * PASSES * P], U32, name=f"w_c{q}", align_bytes=64) for q in range(ROW_TILES)]
-        w_s = [keep.tile([P, 2 * PASSES * P], U8, name=f"w_s{q}", align_bytes=64) for q in range(ROW_TILES)]
         page = [keep.tile([P, T2], F32, name=f"page{q}") for q in range(ROW_TILES)]
-        wgs_t = keep.tile([P, S], F32, name="wgs_t", tag="wide")
+        wgs_t = keep.tile([P, S], F32, name="wgs_t", tag="wgs_then_control")
         factor_rows = keep.tile([P, P], F32, name="factor_rows")
         factors = keep.tile([P, 2 * ROW_TILES], F32, name="factors")
         sc_t = factors[:, 0:ROW_TILES]
@@ -70,17 +73,20 @@ def tile_list_trap_catch_board_kernel(
         def list_half(idx, hf):
             return idx[:, hf * LIST_COLS : (hf + 1) * LIST_COLS]
 
-        def load_scale_rows(queue, plane, scales):
-            rows = plane[:].bitcast(I32).rearrange("p (a c) -> p a c", a=scales.shape[0])
-            for quad in range(QUADS):
-                src = scales[:, 4 * quad : 4 * quad + 4, :].bitcast(I32).rearrange("a r c -> r a c")
-                queue.dma_start(out=rows[32 * quad : 32 * quad + 4], in_=src)
+        def spent_piece(n, a, q):
+            return raw[n, a, q].rearrange("p i c -> p (i c)")
+
+        def load_scale_rows(scale_tile, scales):
+            rows = scale_tile[:].bitcast(I32).rearrange("p (a c) -> p a c", a=scales.shape[0])
+            for s in range(SCALE_ROWS):
+                src = scales[:, s : scales.shape[1] : SCALE_ROWS, :].bitcast(I32).rearrange("a quad c -> quad a c")
+                nc.sync.dma_start(out=rows[s:P:QUADRANT], in_=src)
 
         def load_weight(n, first, count):
             for a in range(PASSES):
                 staged = keep.tile([P, PACK, count * P], F32, name=f"raw{n}_{a}_{first}")
                 src = (w1, w3)[n][a * P * PACK : (a + 1) * P * PACK, first * P : (first + count) * P]
-                nc.sync.dma_start(out=staged[:], in_=src.rearrange("(p i) r -> p i r", i=PACK))
+                nc.sync.dma_start(out=staged[:], in_=src.rearrange("(p i) c -> p i c", i=PACK))
                 for q in range(count):
                     raw[n, a, first + q] = staged[:, :, q * P : (q + 1) * P]
 
@@ -95,15 +101,16 @@ def tile_list_trap_catch_board_kernel(
         nc.gpsimd.memset(w4_s[:].bitcast(I32), 0)
         nc.gpsimd.memset(factor_rows[:], 0.0)
         make_identity(nc, ident[:])
+
         nc.sync.dma_start(idx_tab[:], offs)
         load_table(0)
-        load_scale_rows(nc.sync, tab_s, tab_scales)
+        load_scale_rows(tab_s, tab_scales)
         load_table(1)
         nc.sync.dma_start(
             out=w2_w[:].bitcast(I32).rearrange("p (a c) -> p a c", a=PASSES),
             in_=w2_words.bitcast(I32).rearrange("a p c -> p a c"),
         )
-        load_scale_rows(nc.sync, w2_s, w2_scales)
+        load_scale_rows(w2_s, w2_scales)
         load_weight(0, 0, 2)
         load_weight(1, 0, 1)
         nc.sync.dma_start(out=wgs_t[:, half(0)], in_=wgs[:, half(0)])
@@ -121,50 +128,59 @@ def tile_list_trap_catch_board_kernel(
             load_page(q)
         nc.sync.dma_start(idx_ctl[:], offs4)
         nc.sync.dma_start(out=w4_w[:].bitcast(I32), in_=w4_words[0].bitcast(I32))
-        load_scale_rows(nc.sync, w4_s, w4_scales)
+        load_scale_rows(w4_s, w4_scales)
+
+        def grouped_tile(columns):
+            return ring.tile([P, columns * PACK], BF16, name="grouped", align_bytes=64, bufs=3)
+
+        def interleave(grouped, rows):
+            nc.scalar.copy(
+                out=grouped.rearrange("p (c k i) -> p c i k", k=RUN, i=PACK),
+                in_=rows.rearrange("p i (c k) -> p c i k", k=RUN),
+            )
 
         def quantize_weights(q, first, count):
-            grouped = ring.tile([P, count * P * PACK], BF16, name="grouped", align_bytes=64, bufs=3)
+            grouped = grouped_tile(count * P)
             for piece in range(count):
                 n, a = divmod(first + piece, PASSES)
-                values = grouped[:, piece * PACK * P : (piece + 1) * PACK * P]
-                nc.scalar.copy(
-                    out=values.rearrange("p (c k i) -> p c i k", k=4, i=PACK),
-                    in_=raw[n, a, q].rearrange("p i (c k) -> p c i k", k=4),
-                )
+                interleave(grouped[:, piece * PACK * P : (piece + 1) * PACK * P], raw[n, a, q])
             words = slice(first * P, (first + count) * P)
             nc.vector.quantize_mx(out=w_c[q][:, words].bitcast(FP8X4), scales=w_s[q][:, words], in_=grouped[:])
 
-        def gather_words(a, hf):
-            nc.vector.tensor_copy(v_w[a][:, half(hf)], tab_w[a][:].bitcast(U32).indirect(list_half(idx_tab, hf)))
-
-        def gather_scales(a, hf):
-            nc.vector.tensor_copy(v_s[a][:, half(hf)], tab_s[:, a * T : (a + 1) * T].indirect(list_half(idx_tab, hf)))
-
         for hf in range(2):
             for a in range(PASSES):
-                gather_words(a, hf)
-                gather_scales(a, hf)
+                entries = list_half(idx_tab, hf)
+                nc.vector.tensor_copy(v_w[a][:, half(hf)], tab_w[a][:].bitcast(U32).indirect(entries))
+                nc.vector.tensor_copy(v_s[a][:, half(hf)], tab_s[:, a * T : (a + 1) * T].indirect(entries))
             if hf == 0:
-                for piece in range(2 * PASSES):
+                for piece in range(PIECES):
                     quantize_weights(0, piece, 1)
 
-        def product(u, tag, moving):
-            hf = u % 2
+        def quantised(n, q):
+            pieces = [slice((n * PASSES + a) * P, (n * PASSES + a + 1) * P) for a in range(PASSES)]
+            return [(w_c[q][:, cols].bitcast(FP8X4), w_s[q][:, cols]) for cols in pieces]
+
+        def packed_w2(q):
+            starts = [a * H + q * P for a in range(PASSES)]
+            return [(w2_w[:, 2 * c0 : 2 * (c0 + P)].bitcast(FP4X4), w2_s[:, c0 : c0 + P]) for c0 in starts]
+
+        def product(tag, weight, hf):
             bank = psum.tile([P, HALF], F32, name=tag, tag=tag)
-            for a in range(PASSES):
-                codes, scales = moving(a)
-                if u == 0:
-                    nc.tensor.matmul_mx(
-                        out=bank[:],
-                        lhsT=codes,
-                        lhsT_scale=scales,
-                        rhs=v_w[a][:, half(hf)].bitcast(FP8X4),
-                        rhs_scale=v_s[a][:, half(hf)],
-                        start=(a == 0),
-                        stop=(a == PASSES - 1),
-                    )
-                    continue
+            for a, (codes, scales) in enumerate(weight):
+                nc.tensor.matmul_mx(
+                    out=bank[:],
+                    lhsT=codes,
+                    lhsT_scale=scales,
+                    rhs=v_w[a][:, half(hf)].bitcast(FP8X4),
+                    rhs_scale=v_s[a][:, half(hf)],
+                    start=(a == 0),
+                    stop=(a == PASSES - 1),
+                )
+            return bank
+
+        def product_turned(tag, weight, hf):
+            bank = psum.tile([P, HALF], F32, name=tag, tag=tag)
+            for a, (codes, scales) in enumerate(weight):
                 for jt in range(HALF // P):
                     cols = slice(hf * HALF + jt * P, hf * HALF + (jt + 1) * P)
                     nc.tensor.matmul_mx(
@@ -178,42 +194,38 @@ def tile_list_trap_catch_board_kernel(
                     )
             return bank
 
-        def first_stage(u):
-            q = u // 2
+        def larger_and_third(u, multiply, a2_sb):
+            q, hf = divmod(u, 2)
+            a2 = multiply("a2", packed_w2(q), hf)
+            a1 = multiply("a1", quantised(0, q), hf)
+            a3 = multiply("a3", quantised(1, q), hf)
+            larger = ring.tile([P, HALF], F32, name="larger")
+            nc.scalar.copy(out=a2_sb, in_=a2[:])
+            nc.vector.tensor_tensor(larger[:], a1[:], a2_sb, ALU.max)
+            return larger[:], a3[:]
 
-            def quantised(n):
-                def moving(a):
-                    cols = slice((n * PASSES + a) * P, (n * PASSES + a + 1) * P)
-                    return w_c[q][:, cols].bitcast(FP8X4), w_s[q][:, cols]
+        def first_h():
+            h = ring.tile([P, HALF], F32, name="a3_sb")[:]
+            larger, a3 = larger_and_third(0, product, spent_piece(1, 0, 0))
+            nc.vector.tensor_tensor(h, larger, a3, ALU.subtract)
+            return h
 
-                return moving
-
-            def packed(a):
-                c0 = a * H + q * P
-                return w2_w[:, 2 * c0 : 2 * (c0 + P)].bitcast(FP4X4), w2_s[:, c0 : c0 + P]
-
-            if u % 2 == 0 and q > 0:
+        def turned_terms(u):
+            q, hf = divmod(u, 2)
+            if hf == 0:
                 a2_sb = due[q - 1][:, half(0)]
                 a3_sb = bounded[q - 1][:, half(0)]
             elif q == 0:
-                a2_sb = raw[1, u, 0].rearrange("p i r -> p (i r)")
+                a2_sb = spent_piece(1, PASSES - 1, 0)
                 a3_sb = ring.tile([P, HALF], F32, name="a3_sb")[:]
             else:
                 a2_sb = ring.tile([P, HALF], F32, name="a2_sb")[:]
                 a3_sb = ring.tile([P, HALF], F32, name="a3_sb")[:]
-            a2 = product(u, "a2", packed)
-            a1 = product(u, "a1", quantised(0))
-            a3 = product(u, "a3", quantised(1))
-            larger = ring.tile([P, HALF], F32, name="larger")
-            nc.scalar.copy(out=a2_sb, in_=a2[:])
-            nc.vector.tensor_tensor(larger[:], a1[:], a2_sb, ALU.max)
-            if u == 0:
-                nc.vector.tensor_tensor(a3_sb, larger[:], a3[:], ALU.subtract)
-                return a3_sb
-            nc.scalar.activation(a3_sb, a3[:], ACT.Copy, scale=-1.0)
-            return a3_sb, larger[:]
+            larger, a3 = larger_and_third(u, product_turned, a2_sb)
+            nc.scalar.activation(a3_sb, a3, ACT.Copy, scale=-1.0)
+            return a3_sb, larger
 
-        def turn(u, terms):
+        def turn_back(u, terms):
             q, hf = divmod(u, 2)
             bank = psum.tile([P, HALF], F32, name="h", tag="h")
             for n, term in enumerate(terms):
@@ -221,10 +233,10 @@ def tile_list_trap_catch_board_kernel(
                     cols = slice(jt * P, (jt + 1) * P)
                     nc.tensor.matmul(
                         bank[:, cols], term[:, cols], ident[:], is_transpose=True,
-                        start=(n == 0 and jt == 0), stop=(n == 1 and jt == HALF // P - 1),
+                        start=(n == 0 and jt == 0), stop=(n == len(terms) - 1 and jt == HALF // P - 1),
                     )
             if hf == 1 and q + 1 < ROW_TILES:
-                h = raw[1, PASSES - 1, q + 1].rearrange("p i r -> p (i r)")
+                h = spent_piece(1, PASSES - 1, q + 1)
             else:
                 h = ring.tile([P, HALF], F32, name="h_sb")[:]
             nc.scalar.copy(out=h, in_=bank[:])
@@ -234,56 +246,58 @@ def tile_list_trap_catch_board_kernel(
             q, hf = divmod(u, 2)
             nc.vector.tensor_tensor(page[q][:].indirect(list_half(idx_put, hf)), h, wgs_t[:, half(hf)], ALU.mult)
 
-        def fetch_due(q, cols, idx):
-            nc.vector.tensor_copy(due[q][:, cols], page[q][:].indirect(idx))
+        def turn_factors():
+            turned = psum.tile([P, HALF], F32, name="h", tag="h")
+            nc.tensor.transpose(turned[:, 0:P], factor_rows[:], ident[:])
+            nc.scalar.copy(out=factors[:], in_=turned[:, 0 : 2 * ROW_TILES])
 
-        def bound(q, cols):
-            x_nat = ring.tile([P, M], BF16, name="x_nat")
+        def fetch_due(q, cols, entries):
+            nc.vector.tensor_copy(due[q][:, cols], page[q][:].indirect(entries))
+
+        def make_x(q, cols):
+            x_tile = ring.tile([P, M], BF16, name="x_tile")
             nc.scalar.activation(bounded[q][:, cols], due[q][:, cols], ACT.Tanh, scale=sc_t[:, q : q + 1])
-            nc.scalar.activation(x_nat[:, cols], bounded[q][:, cols], ACT.Copy, scale=gain_t[:, q : q + 1])
+            nc.scalar.activation(x_tile[:, cols], bounded[q][:, cols], ACT.Copy, scale=gain_t[:, q : q + 1])
             for hf in range(cols.start // HALF, cols.stop // HALF):
-                for i in range(PACK):
-                    nc.sync.dma_start(out=x_rows[hf][32 * q : 32 * (q + 1), i, :], in_=x_nat[i:P:PACK, half(hf)])
+                rows = slice(q * P // PACK, (q + 1) * P // PACK)
+                nc.sync.dma_start(out=x_rows[hf][rows], in_=x_tile[:, half(hf)])
 
-        terms = first_stage(0)
+        h_first = first_h()
+        terms = None
         for u in range(UNITS):
             q, hf = divmod(u, 2)
             if q == 0:
                 quantize_weights(1, hf * PASSES, PASSES)
             elif hf == 0 and q + 1 < ROW_TILES:
-                quantize_weights(q + 1, 0, 2 * PASSES)
-            ahead = first_stage(u + 1) if u + 1 < UNITS else None
-            put(u, terms if u == 0 else turn(u, terms))
-            if u == 1:
-                turned = psum.tile([P, HALF], F32, name="h", tag="h")
-                nc.tensor.transpose(turned[:, 0:P], factor_rows[:], ident[:])
-                nc.scalar.copy(out=factors[:], in_=turned[:, 0 : 2 * ROW_TILES])
+                quantize_weights(q + 1, 0, PIECES)
+            ahead = turned_terms(u + 1) if u + 1 < UNITS else None
+            put(u, h_first if u == 0 else turn_back(u, terms))
             terms = ahead
+            if u == 1:
+                turn_factors()
             if hf == 1 and q + 1 < ROW_TILES:
                 fetch_due(q, slice(0, M), idx_due[:])
             if hf == 0 and q > 0:
-                bound(q - 1, slice(0, M))
+                make_x(q - 1, slice(0, M))
         for hf in range(2):
             fetch_due(ROW_TILES - 1, half(hf), list_half(idx_due, hf))
-            bound(ROW_TILES - 1, half(hf))
+            make_x(ROW_TILES - 1, half(hf))
 
-        control = keep.tile([P, 2 * ROW_TILES, HALF], F32, name="control", tag="wide")
-        x_c, x_s = [], []
+        control = keep.tile([P, UNITS, HALF], F32, name="control", tag="wgs_then_control")
+        x_c, x_s, x_grouped = [], [], []
         for hf in range(2):
-            x_grouped = ring.tile([P, HALF, PACK], BF16, name="grouped", align_bytes=64, bufs=3)
-            nc.scalar.copy(
-                out=x_grouped[:].rearrange("p (c k) i -> p c i k", k=4),
-                in_=x_rows[hf][:].rearrange("p i (c k) -> p c i k", k=4),
-            )
+            x_grouped.append(grouped_tile(HALF))
+            interleave(x_grouped[hf][:], x_rows[hf][:])
             x_c.append(ring.tile([P, HALF], U32, name="x_c", align_bytes=64))
             x_s.append(ring.tile([P, HALF], U8, name="x_s", align_bytes=64))
-            nc.vector.quantize_mx(
-                out=x_c[hf][:].bitcast(FP8X4), scales=x_s[hf][:], in_=x_grouped[:].rearrange("p c i -> p (c i)")
-            )
-        sizes = keep.tile([P, 2 * ROW_TILES, HALF], F32, name="sizes", tag="x_rows0")
+            nc.vector.quantize_mx(out=x_c[hf][:].bitcast(FP8X4), scales=x_s[hf][:], in_=x_grouped[hf][:])
+        sizes = keep.tile([P, UNITS, HALF], F32, name="sizes", tag="x_rows0")
         for hf in range(2):
             for q in range(ROW_TILES):
-                picked = control[:, hf * ROW_TILES + q, :]
+                if hf == 1 and q == ROW_TILES - 1:
+                    picked = x_grouped[0][:].bitcast(F32)[:, 0:HALF]
+                else:
+                    picked = control[:, hf * ROW_TILES + q, :]
                 nc.vector.tensor_copy(picked, page[q][:].indirect(list_half(idx_ctl, hf)))
                 size = sizes[:, hf * ROW_TILES + q, :]
                 nc.scalar.activation(size, picked, ACT.Abs, scale=sc_t[:, q : q + 1])

from contextlib import ExitStack

import concourse.mybir as mybir
from concourse.masks import make_identity

K, H, T, S, T2, M = 1024, 512, 4096, 1024, 2048, 1024
FLOPS = 3 * 2 * K * H * S + 2 * H * H * M

F32 = mybir.dt.float32
BF16 = mybir.dt.bfloat16
I32 = mybir.dt.int32
U32 = mybir.dt.uint32
U16 = mybir.dt.uint16
U8 = mybir.dt.uint8
FP8X4 = mybir.dt.float8_e4m3fn_x4
FP4X4 = mybir.dt.float4_e2m1fn_x4
ALU = mybir.AluOpType
ACT = mybir.ActivationFunctionType

P = 128
PACK = 4
PASSES = K // (P * PACK)
QUADRANT = 32
SCALE_ROWS = 4
ROW_TILES = H // P
HALF = 512
LIST_COLS = HALF // 16
UNITS = 2 * ROW_TILES
PIECES = 2 * PASSES
RUN = 4


def tile_list_trap_catch_board_kernel(
    tc, tab_words, tab_scales, offs, offs2, offs3, offs4, w1, w2_words, w2_scales, w3, wgs, page0, sc, gain,
    w4_words, w4_scales, out,
):
    nc = tc.nc
    with ExitStack() as ctx:
        keep = ctx.enter_context(tc.tile_pool(name="keep", bufs=1))
        ring = ctx.enter_context(tc.tile_pool(name="ring", bufs=2))
        psum = ctx.enter_context(tc.psum_pool(name="psum", bufs=2))

        idx_tab = keep.tile([P, S // 16], U16, name="idx_tab")
        idx_put = keep.tile([P, S // 16], U16, name="idx_put")
        idx_due = keep.tile([P, M // 16], U16, name="idx_due")
        idx_ctl = keep.tile([P, M // 16], U16, name="idx_ctl")

        tab_w = [keep.tile([P, T], I32, name=f"tab_w{a}") for a in range(PASSES)]
        tab_s = keep.tile([P, PASSES * T], U8, name="tab_s")
        v_w = [keep.tile([P, S], U32, name=f"v_w{a}", align_bytes=64) for a in range(PASSES)]
        v_s = [keep.tile([P, S], U8, name=f"v_s{a}", align_bytes=64) for a in range(PASSES)]
        w2_w = keep.tile([P, PASSES * 2 * H], U8, name="w2_w", align_bytes=64)
        w2_s = keep.tile([P, PASSES * H], U8, name="w2_s", align_bytes=64)
        w4_w = keep.tile([P, 2 * H], U8, name="w4_w", align_bytes=64)
        w4_s = keep.tile([P, H], U8, name="w4_s", align_bytes=64)
        w_c = [keep.tile([P, PIECES * P], U32, name=f"w_c{q}", align_bytes=64) for q in range(ROW_TILES)]
        w_s = [keep.tile([P, PIECES * P], U8, name=f"w_s{q}", align_bytes=64) for q in range(ROW_TILES)]
        raw = {}
        page = [keep.tile([P, T2], F32, name=f"page{q}") for q in range(ROW_TILES)]
        wgs_t = keep.tile([P, S], F32, name="wgs_t", tag="wgs_then_control")
        factor_rows = keep.tile([P, P], F32, name="factor_rows")
        factors = keep.tile([P, 2 * ROW_TILES], F32, name="factors")
        sc_t = factors[:, 0:ROW_TILES]
        gain_t = factors[:, ROW_TILES : 2 * ROW_TILES]
        ident = keep.tile([P, P], F32, name="ident")
        due = [keep.tile([P, M], F32, name=f"due{q}") for q in range(ROW_TILES)]
        bounded = [keep.tile([P, M], F32, name=f"bounded{q}") for q in range(ROW_TILES)]
        x_rows = [keep.tile([P, PACK, HALF], BF16, name=f"x_rows{hf}", tag=f"x_rows{hf}") for hf in range(2)]

        def half(hf):
            return slice(hf * HALF, (hf + 1) * HALF)

        def list_half(idx, hf):
            return idx[:, hf * LIST_COLS : (hf + 1) * LIST_COLS]

        def spent_piece(n, a, q):
            return raw[n, a, q].rearrange("p i c -> p (i c)")

        def load_scale_rows(scale_tile, scales):
            rows = scale_tile[:].bitcast(I32).rearrange("p (a c) -> p a c", a=scales.shape[0])
            for s in range(SCALE_ROWS):
                src = scales[:, s : scales.shape[1] : SCALE_ROWS, :].bitcast(I32).rearrange("a quad c -> quad a c")
                nc.sync.dma_start(out=rows[s:P:QUADRANT], in_=src)

        def load_weight(n, first, count):
            for a in range(PASSES):
                staged = keep.tile([P, PACK, count * P], F32, name=f"raw{n}_{a}_{first}")
                src = (w1, w3)[n][a * P * PACK : (a + 1) * P * PACK, first * P : (first + count) * P]
                nc.sync.dma_start(out=staged[:], in_=src.rearrange("(p i) c -> p i c", i=PACK))
                for q in range(count):
                    raw[n, a, first + q] = staged[:, :, q * P : (q + 1) * P]

        def load_table(a):
            nc.sync.dma_start(out=tab_w[a][:], in_=tab_words[a].rearrange("p t i -> p (t i)").bitcast(I32))

        def load_page(q):
            nc.sync.dma_start(out=page[q][:], in_=page0[q * P : (q + 1) * P, :])

        nc.vector.memset(tab_s[:].bitcast(I32), 0)
        nc.gpsimd.memset(w2_s[:].bitcast(I32), 0)
        nc.gpsimd.memset(w4_s[:].bitcast(I32), 0)
        nc.gpsimd.memset(factor_rows[:], 0.0)
        make_identity(nc, ident[:])

        nc.sync.dma_start(idx_tab[:], offs)
        load_table(0)
        load_scale_rows(tab_s, tab_scales)
        load_table(1)
        nc.sync.dma_start(
            out=w2_w[:].bitcast(I32).rearrange("p (a c) -> p a c", a=PASSES),
            in_=w2_words.bitcast(I32).rearrange("a p c -> p a c"),
        )
        load_scale_rows(w2_s, w2_scales)
        load_weight(0, 0, 2)
        load_weight(1, 0, 1)
        nc.sync.dma_start(out=wgs_t[:, half(0)], in_=wgs[:, half(0)])
        nc.sync.dma_start(idx_put[:], offs2)
        load_page(0)
        load_weight(1, 1, 1)
        nc.sync.dma_start(out=wgs_t[:, half(1)], in_=wgs[:, half(1)])
        nc.sync.dma_start(idx_due[:], offs3)
        nc.sync.dma_start(out=factor_rows[0:ROW_TILES, :], in_=sc.rearrange("(q p) -> q p", p=P))
        nc.sync.dma_start(out=factor_rows[ROW_TILES : 2 * ROW_TILES, :], in_=gain.rearrange("(q p) -> q p", p=P))
        for q in range(1, ROW_TILES):
            if q + 1 < ROW_TILES:
                load_weight(0, q + 1, 1)
                load_weight(1, q + 1, 1)
            load_page(q)
        nc.sync.dma_start(idx_ctl[:], offs4)
        nc.sync.dma_start(out=w4_w[:].bitcast(I32), in_=w4_words[0].bitcast(I32))
        load_scale_rows(w4_s, w4_scales)

        def grouped_tile(columns):
            return ring.tile([P, columns * PACK], BF16, name="grouped", align_bytes=64, bufs=3)

        def interleave(grouped, rows):
            nc.scalar.copy(
                out=grouped.rearrange("p (c k i) -> p c i k", k=RUN, i=PACK),
                in_=rows.rearrange("p i (c k) -> p c i k", k=RUN),
            )

        def quantize_weights(q, first, count):
            grouped = grouped_tile(count * P)
            for piece in range(count):
                n, a = divmod(first + piece, PASSES)
                interleave(grouped[:, piece * PACK * P : (piece + 1) * PACK * P], raw[n, a, q])
            words = slice(first * P, (first + count) * P)
            nc.vector.quantize_mx(out=w_c[q][:, words].bitcast(FP8X4), scales=w_s[q][:, words], in_=grouped[:])

        for hf in range(2):
            for a in range(PASSES):
                entries = list_half(idx_tab, hf)
                nc.vector.tensor_copy(v_w[a][:, half(hf)], tab_w[a][:].bitcast(U32).indirect(entries))
                nc.vector.tensor_copy(v_s[a][:, half(hf)], tab_s[:, a * T : (a + 1) * T].indirect(entries))
            if hf == 0:
                for piece in range(PIECES):
                    quantize_weights(0, piece, 1)

        def quantised(n, q):
            pieces = [slice((n * PASSES + a) * P, (n * PASSES + a + 1) * P) for a in range(PASSES)]
            return [(w_c[q][:, cols].bitcast(FP8X4), w_s[q][:, cols]) for cols in pieces]

        def packed_w2(q):
            starts = [a * H + q * P for a in range(PASSES)]
            return [(w2_w[:, 2 * c0 : 2 * (c0 + P)].bitcast(FP4X4), w2_s[:, c0 : c0 + P]) for c0 in starts]

        def product(tag, weight, hf):
            bank = psum.tile([P, HALF], F32, name=tag, tag=tag)
            for a, (codes, scales) in enumerate(weight):
                nc.tensor.matmul_mx(
                    out=bank[:],
                    lhsT=codes,
                    lhsT_scale=scales,
                    rhs=v_w[a][:, half(hf)].bitcast(FP8X4),
                    rhs_scale=v_s[a][:, half(hf)],
                    start=(a == 0),
                    stop=(a == PASSES - 1),
                )
            return bank

        def product_turned(tag, weight, hf):
            bank = psum.tile([P, HALF], F32, name=tag, tag=tag)
            for a, (codes, scales) in enumerate(weight):
                for jt in range(HALF // P):
                    cols = slice(hf * HALF + jt * P, hf * HALF + (jt + 1) * P)
                    nc.tensor.matmul_mx(
                        out=bank[:, jt * P : (jt + 1) * P],
                        lhsT=v_w[a][:, cols].bitcast(FP8X4),
                        lhsT_scale=v_s[a][:, cols],
                        rhs=codes,
                        rhs_scale=scales,
                        start=(a == 0 and jt == 0),
                        stop=(a == PASSES - 1 and jt == HALF // P - 1),
                    )
            return bank

        def larger_and_third(u, multiply, a2_sb):
            q, hf = divmod(u, 2)
            a2 = multiply("a2", packed_w2(q), hf)
            a1 = multiply("a1", quantised(0, q), hf)
            a3 = multiply("a3", quantised(1, q), hf)
            larger = ring.tile([P, HALF], F32, name="larger")
            nc.scalar.copy(out=a2_sb, in_=a2[:])
            nc.vector.tensor_tensor(larger[:], a1[:], a2_sb, ALU.max)
            return larger[:], a3[:]

        def first_h():
            h = ring.tile([P, HALF], F32, name="a3_sb")[:]
            larger, a3 = larger_and_third(0, product, spent_piece(1, 0, 0))
            nc.vector.tensor_tensor(h, larger, a3, ALU.subtract)
            return h

        def turned_terms(u):
            q, hf = divmod(u, 2)
            if hf == 0:
                a2_sb = due[q - 1][:, half(0)]
                a3_sb = bounded[q - 1][:, half(0)]
            elif q == 0:
                a2_sb = spent_piece(1, PASSES - 1, 0)
                a3_sb = ring.tile([P, HALF], F32, name="a3_sb")[:]
            else:
                a2_sb = ring.tile([P, HALF], F32, name="a2_sb")[:]
                a3_sb = ring.tile([P, HALF], F32, name="a3_sb")[:]
            larger, a3 = larger_and_third(u, product_turned, a2_sb)
            nc.scalar.activation(a3_sb, a3, ACT.Copy, scale=-1.0)
            return a3_sb, larger

        def turn_back(u, terms):
            q, hf = divmod(u, 2)
            bank = psum.tile([P, HALF], F32, name="h", tag="h")
            for n, term in enumerate(terms):
                for jt in range(HALF // P):
                    cols = slice(jt * P, (jt + 1) * P)
                    nc.tensor.matmul(
                        bank[:, cols], term[:, cols], ident[:], is_transpose=True,
                        start=(n == 0 and jt == 0), stop=(n == len(terms) - 1 and jt == HALF // P - 1),
                    )
            if hf == 1 and q + 1 < ROW_TILES:
                h = spent_piece(1, PASSES - 1, q + 1)
            else:
                h = ring.tile([P, HALF], F32, name="h_sb")[:]
            nc.scalar.copy(out=h, in_=bank[:])
            return h

        def put(u, h):
            q, hf = divmod(u, 2)
            nc.vector.tensor_tensor(page[q][:].indirect(list_half(idx_put, hf)), h, wgs_t[:, half(hf)], ALU.mult)

        def turn_factors():
            turned = psum.tile([P, HALF], F32, name="h", tag="h")
            nc.tensor.transpose(turned[:, 0:P], factor_rows[:], ident[:])
            nc.scalar.copy(out=factors[:], in_=turned[:, 0 : 2 * ROW_TILES])

        def fetch_due(q, cols, entries):
            nc.vector.tensor_copy(due[q][:, cols], page[q][:].indirect(entries))

        def make_x(q, cols):
            x_tile = ring.tile([P, M], BF16, name="x_tile")
            nc.scalar.activation(bounded[q][:, cols], due[q][:, cols], ACT.Tanh, scale=sc_t[:, q : q + 1])
            nc.scalar.activation(x_tile[:, cols], bounded[q][:, cols], ACT.Copy, scale=gain_t[:, q : q + 1])
            for hf in range(cols.start // HALF, cols.stop // HALF):
                rows = slice(q * P // PACK, (q + 1) * P // PACK)
                nc.sync.dma_start(out=x_rows[hf][rows], in_=x_tile[:, half(hf)])

        h_first = first_h()
        terms = None
        for u in range(UNITS):
            q, hf = divmod(u, 2)
            if q == 0:
                quantize_weights(1, hf * PASSES, PASSES)
            elif hf == 0 and q + 1 < ROW_TILES:
                quantize_weights(q + 1, 0, PIECES)
            ahead = turned_terms(u + 1) if u + 1 < UNITS else None
            put(u, h_first if u == 0 else turn_back(u, terms))
            terms = ahead
            if u == 1:
                turn_factors()
            if hf == 1 and q + 1 < ROW_TILES:
                fetch_due(q, slice(0, M), idx_due[:])
            if hf == 0 and q > 0:
                make_x(q - 1, slice(0, M))
        for hf in range(2):
            fetch_due(ROW_TILES - 1, half(hf), list_half(idx_due, hf))
            make_x(ROW_TILES - 1, half(hf))

        control = keep.tile([P, UNITS, HALF], F32, name="control", tag="wgs_then_control")
        x_c, x_s, x_grouped = [], [], []
        for hf in range(2):
            x_grouped.append(grouped_tile(HALF))
            interleave(x_grouped[hf][:], x_rows[hf][:])
            x_c.append(ring.tile([P, HALF], U32, name="x_c", align_bytes=64))
            x_s.append(ring.tile([P, HALF], U8, name="x_s", align_bytes=64))
            nc.vector.quantize_mx(out=x_c[hf][:].bitcast(FP8X4), scales=x_s[hf][:], in_=x_grouped[hf][:])
        sizes = keep.tile([P, UNITS, HALF], F32, name="sizes", tag="x_rows0")
        for hf in range(2):
            for q in range(ROW_TILES):
                if hf == 1 and q == ROW_TILES - 1:
                    picked = x_grouped[0][:].bitcast(F32)[:, 0:HALF]
                else:
                    picked = control[:, hf * ROW_TILES + q, :]
                nc.vector.tensor_copy(picked, page[q][:].indirect(list_half(idx_ctl, hf)))
                size = sizes[:, hf * ROW_TILES + q, :]
                nc.scalar.activation(size, picked, ACT.Abs, scale=sc_t[:, q : q + 1])
                tag = ("a2", "a1", "a3", "h")[q]
                y = psum.tile([P, HALF], F32, name=tag, tag=tag)
                nc.tensor.matmul_mx(
                    out=y[:],
                    lhsT=w4_w[:, 2 * q * P : 2 * (q + 1) * P].bitcast(FP4X4),
                    lhsT_scale=w4_s[:, q * P : (q + 1) * P],
                    rhs=x_c[hf][:].bitcast(FP8X4),
                    rhs_scale=x_s[hf][:],
                    start=True,
                    stop=True,
                )
                nc.vector.tensor_tensor(picked, y[:], size, ALU.subtract)
                nc.sync.dma_start(out=out[q * P : (q + 1) * P, half(hf)], in_=picked)
